import numpy as np
import ml_dtypes


def mxq(x, axis, fmt="e4m3"):
    dtype, down = {"e4m3": (ml_dtypes.float8_e4m3fn, 7), "e5m2": (ml_dtypes.float8_e5m2, 14)}[fmt]
    v = np.moveaxis(np.asarray(x, np.float32).astype(ml_dtypes.bfloat16).astype(np.float64), axis, -1)
    blocks = v.reshape(v.shape[:-1] + (-1, 32))
    amax = np.abs(blocks).max(-1, keepdims=True)
    byte = np.maximum(np.where(amax > 0, np.frexp(amax)[1] - 1 + 127, 0) - down, 1)
    scale = np.exp2(byte - 127.0)
    codes = (blocks / scale).astype(np.float32).astype(dtype).astype(np.float64)
    return np.moveaxis((codes * scale).reshape(v.shape), -1, axis)


WIDE = False


def mx_kscale(k):
    if not WIDE:
        return np.ones(k)
    levels = np.array([10, -10, 5, -5, 0])
    if k % 512:
        return np.exp2(np.random.permutation(np.resize(levels, k // 32))).repeat(32)
    a = np.empty((k // 512, 16))
    for p in range(k // 512):
        a[p, :8] = np.random.permutation(np.resize(levels, 8))
        for g in range(8):
            far = levels[np.abs(levels - a[p, g]) >= 10]
            a[p, g + 8] = far[np.random.randint(len(far))]
    return np.exp2(a.ravel()).repeat(32)


def f64(x):
    return np.asarray(x).astype(np.float64)


def striped(idx):
    return np.tile(idx.reshape(-1, 16).T, (8, 1)).astype(np.uint16)


def unstriped(offs):
    return offs[:16].T.reshape(-1).astype(np.int64)


def striped8(idx):
    return np.concatenate([x.reshape(-1, 16).T for x in idx]).astype(np.uint16)


def runs(offs, k):
    lists = np.stack([offs[16 * r : 16 * r + 16].T.reshape(-1) for r in range(8)]).astype(np.int64)
    return lists[np.arange(k) % 512 // 64]


def pack_weight(w):
    k, n = w.shape
    w = f64(np.asarray(w, np.float32).astype(ml_dtypes.bfloat16)).reshape(k // 32, 32, n)
    amax = np.abs(w).max(1)
    byte = np.clip(np.where(amax > 0, np.frexp(amax)[1] - 1 + 127 - 7, 1), 1, 254)
    scaled = (w * np.exp2(127.0 - byte)[:, None, :]).reshape(k, n).astype(np.float32)
    words = np.ascontiguousarray(scaled.reshape(k // 512, 128, 4, n).transpose(0, 1, 3, 2)).astype(ml_dtypes.float8_e4m3fn).view(np.uint8)
    return words, np.ascontiguousarray(byte.astype(np.uint8).reshape(k // 512, 16, n))


def unpack_weight(words, scales):
    g, p, n, _ = words.shape
    vals = np.ascontiguousarray(words).view(ml_dtypes.float8_e4m3fn).astype(np.float64) * np.repeat(np.exp2(scales.astype(np.float64) - 127.0), 8, axis=1)[..., None]
    return vals.transpose(0, 1, 3, 2).reshape(g * 512, n)


K, T, S, N, H = 512, 2048, 512, 512, 512


def setup_inputs():
    n = np.random.standard_normal
    s = mx_kscale(K)[:, None]
    u = mx_kscale(H)
    packed_xT = pack_weight(n((K, T)) * s)
    return {
        "x_words": packed_xT[0],
        "x_scales": packed_xT[1],
        "w1": (n((K, H)) / np.sqrt(K) / s).astype(np.float32),
        "w2": (n((K, H)) / np.sqrt(K) / s).astype(np.float32),
        "w3": (n((K, H)) / np.sqrt(K) / s).astype(np.float32),
        "gn": (np.random.uniform(0.5, 1.5, (H, 1)) * u[:, None]).astype(np.float32),
        "w4": (n((H, N)) / np.sqrt(H) / u[:, None]).astype(np.float32),
        "offs": striped(np.random.permutation(T)[:S]),
        "two": striped(np.random.permutation(T)[:S]),
        "three": striped(np.random.permutation(T)[:S]),
        "n1": striped8(np.stack([np.random.permutation(S) for _ in range(8)])),
        "n2": striped8(np.stack([np.random.permutation(S) for _ in range(8)])),
        "n3": striped8(np.stack([np.random.permutation(S) for _ in range(8)])),
        "n4": striped8(np.stack([np.random.permutation(S) for _ in range(8)])),
        "n5": striped8(np.stack([np.random.permutation(S) for _ in range(8)])),
        "n6": striped8(np.stack([np.random.permutation(S) for _ in range(8)])),
        "n7": striped8(np.stack([np.random.permutation(S) for _ in range(8)])),
        "n8": striped8(np.stack([np.random.permutation(S) for _ in range(8)])),
    }


def reference(x_words, x_scales, w1, w2, w3, gn, w4, offs, two, three, n1, n2, n3, n4, n5, n6, n7, n8):
    xq = unpack_weight(x_words, x_scales)[:, unstriped(offs)]
    y = mxq(f64(w1), 0, "e4m3").T @ xq
    x_two = unpack_weight(x_words, x_scales)[:, unstriped(two)]
    d = mxq(f64(w2), 0, "e4m3").T @ x_two
    m1 = np.maximum(y[np.arange(H)[:, None], runs(n1, H)] + d[np.arange(H)[:, None], runs(n3, H)], y[np.arange(H)[:, None], runs(n2, H)] + d[np.arange(H)[:, None], runs(n4, H)])
    x_three = unpack_weight(x_words, x_scales)[:, unstriped(three)]
    b = mxq(f64(w3), 0, "e4m3").T @ x_three
    z = f64(gn) * ((m1 - (m1[np.arange(H)[:, None], runs(n5, H)])) / (np.abs(b) + np.abs(b[np.arange(H)[:, None], runs(n6, H)]) + 0.5))
    h = mxq(f64(w4), 0, "e4m3").T @ mxq(z, 0, "e4m3")
    return np.maximum(h[np.arange(N)[:, None], runs(n7, N)], h[np.arange(N)[:, None], runs(n8, N)]) - (0.75 * h)

@@ -1,0 +1,320 @@
+from contextlib import ExitStack
+
+import concourse.mybir as mybir
+from concourse.masks import make_identity
+
+K, T, S, N, H = 512, 2048, 512, 512, 512
+FLOPS = 4 * 2 * 512 * 512 * 512
+
+F32 = mybir.dt.float32
+BF16 = mybir.dt.bfloat16
+I32 = mybir.dt.int32
+U32 = mybir.dt.uint32
+U16 = mybir.dt.uint16
+U8 = mybir.dt.uint8
+FP8X4 = mybir.dt.float8_e4m3fn_x4
+ALU = mybir.AluOpType
+ACT = mybir.ActivationFunctionType
+
+P = 128
+PACK = 4
+HALF = S // 2
+COLS = S // 16
+
+
+def tile_picked_triopathbnormbover_none_p_kernel(tc, x_words, x_scales, w1, w2, w3, gn, w4, offs, two, three, n1, n2, n3, n4, n5, n6, n7, n8, out):
+    nc = tc.nc
+    with ExitStack() as ctx:
+        keep = ctx.enter_context(tc.tile_pool(name="keep", bufs=1))
+        psum = ctx.enter_context(tc.psum_pool(name="psum", bufs=1))
+
+        def sb(name, shape, dtype, tag=None):
+            return keep.tile(shape, dtype, name=name, tag=tag or name, align_bytes=64)
+
+        banks = [psum.tile([P, S], F32, name="bank%d" % i) for i in range(8)]
+        mm_bank = banks[0:2]
+        s1_bank, s2_bank = banks[2], banks[3]
+        num_bank = banks[4:6]
+        den_bank = banks[6:8]
+
+        lists = {}
+
+        def load_list(name, ap):
+            lists[name] = sb("list_" + name, [P, COLS], U16)
+            nc.sync.dma_start(lists[name][:], ap)
+
+        raw = {}
+
+        def load_w(name, ap, parts):
+            width = H // parts
+            raw[name] = [sb("raw_%s_%d" % (name, i), [P, PACK, width], F32) for i in range(parts)]
+            for i in range(parts):
+                nc.sync.dma_start(raw[name][i][:], ap.rearrange("(p j) c -> p j c", j=PACK)[:, :, width * i : width * (i + 1)])
+
+        xs = sb("xs", [P, T], U8)
+        nc.gpsimd.memset(xs[:].bitcast(I32), 0)
+        load_list("offs", offs)
+        load_list("two", two)
+        load_list("three", three)
+        xw = sb("xw", [P, T], I32)
+        nc.sync.dma_start(xw[:], x_words[0].rearrange("p n t -> p (n t)").bitcast(I32))
+        for q in range(4):
+            nc.scalar.dma_start(xs[32 * q : 32 * q + 4, :].bitcast(I32), x_scales[0, 4 * q : 4 * q + 4, :].bitcast(I32))
+        load_w("w1", w1, 2)
+        load_w("w2", w2, 1)
+        load_list("n1", n1)
+        load_list("n2", n2)
+        load_list("n3", n3)
+        load_list("n4", n4)
+        load_w("w3", w3, 1)
+        gain = sb("gain", [P, PACK], F32)
+        nc.sync.dma_start(gain[:], gn.rearrange("(p t) o -> p (t o)", t=PACK))
+        load_list("n6", n6)
+        load_list("n5", n5)
+        load_w("w4", w4, 1)
+        load_list("n7", n7)
+        load_list("n8", n8)
+
+        ident = sb("ident", [P, P], F32)
+        make_identity(nc, ident[:])
+
+        warm = sb("warm", [P, 2], F32)
+        nc.vector.memset(warm[:, 0:1], 1.0)
+        nc.scalar.activation(warm[:, 1:2], warm[:, 0:1], ACT.Abs_reciprocal_sqrt)
+
+        ywin = [sb("ywin%d" % t, [P, 2 * S], F32) for t in range(PACK)]
+        dwin = [sb("dwin%d" % t, [P, 2 * S], F32) for t in range(PACK)]
+        bwin = [sb("bwin%d" % t, [P, 2 * S], F32) for t in range(PACK)]
+
+        xcode, xscale = {}, {}
+
+        def pick_words(name, tag=None):
+            xcode[name] = sb("xc_" + name, [P, S], U32, tag)
+            nc.vector.tensor_copy(xcode[name][:], xw[:].bitcast(U32).indirect(lists[name][:]))
+
+        def pick_bytes(name):
+            xscale[name] = sb("xb_" + name, [P, S], U8)
+            nc.vector.tensor_copy(xscale[name][:], xs[:].indirect(lists[name][:]))
+
+        grouped, wcode, wscale = {}, {}, {}
+
+        def weave(name):
+            grouped[name] = sb("grp_" + name, [P, PACK * H], BF16)
+            dst = grouped[name][:].rearrange("p (t m j) -> p m j t", t=PACK, j=PACK)
+            for i in range(2):
+                if len(raw[name]) == 2:
+                    src = raw[name][i][:].rearrange("p j (m t) -> p m j t", t=PACK)
+                else:
+                    src = raw[name][0][:].rearrange("p j (m t) -> p m j t", t=PACK)[:, 64 * i : 64 * (i + 1)]
+                nc.scalar.copy(dst[:, 64 * i : 64 * (i + 1)], src)
+
+        def quant_w(name, tag=None):
+            wcode[name] = sb("wc_" + name, [P, H], U32, tag)
+            wscale[name] = sb("ws_" + name, [P, H], U8)
+            nc.vector.quantize_mx(out=wcode[name][:].bitcast(FP8X4), scales=wscale[name][:], in_=grouped[name][:])
+
+        def product(bank_ap, wname, t, codes, scales):
+            cols = slice(P * t, P * (t + 1))
+            nc.tensor.matmul_mx(out=bank_ap, lhsT=wcode[wname][:, cols].bitcast(FP8X4), lhsT_scale=wscale[wname][:, cols],
+                                rhs=codes.bitcast(FP8X4), rhs_scale=scales, start=True, stop=True)
+
+        def turn(dst, src, start, stop):
+            nc.tensor.matmul(dst, lhsT=src, rhs=ident[:], start=start, stop=stop, is_transpose=True)
+
+        def blk(ap, b):
+            return ap[:, P * b : P * (b + 1)]
+
+        def fetch(name, win, lname, lo=0, hi=S):
+            nc.vector.tensor_copy(name[:, lo:hi], win[:].indirect(lists[lname][:, lo // 16 : hi // 16]))
+
+        pick_bytes("offs")
+        pick_bytes("two")
+        pick_bytes("three")
+        pick_words("offs")
+        pick_words("two")
+        weave("w1")
+        quant_w("w1")
+        pick_words("three", "raw_w1_1")
+        for t in range(PACK):
+            product(mm_bank[t % 2][:], "w1", t, xcode["offs"][:], xscale["offs"][:])
+            nc.scalar.copy(ywin[t][:, :S], mm_bank[t % 2][:])
+        weave("w2")
+        quant_w("w2")
+        for t in range(PACK):
+            product(mm_bank[t % 2][:], "w2", t, xcode["two"][:], xscale["two"][:])
+            nc.scalar.copy(dwin[t][:, :S], mm_bank[t % 2][:])
+
+        g1 = [sb("g1_%d" % t, [P, S], F32) for t in range(PACK)]
+        g2 = [sb("g2_%d" % t, [P, S], F32) for t in range(PACK)]
+        g3 = [sb("g3_%d" % t, [P, S], F32) for t in range(PACK)]
+        g4 = [sb("g4_%d" % t, [P, S], F32) for t in range(PACK)]
+        g5 = [sb("g5_%d" % t, [P, S], F32) for t in range(PACK)]
+        g6 = [sb("g6_%d" % t, [P, S], F32) for t in range(PACK)]
+        s1t = [sb("s1t_%d" % t, [P, S], F32) for t in range(PACK)]
+        m1t = [sb("m1t_%d" % t, [P, S], F32) for t in range(PACK)]
+        rt = [[sb("rt_%d_%d" % (u, a), [P, S], F32) for a in range(2)] for u in range(2)]
+        rs = [[sb("rs_%d_%d" % (u, a), [P, S], F32) for a in range(2)] for u in range(2)]
+        zt = [[sb("zt_%d_%d" % (u, a), [P, S], BF16) for a in range(2)] for u in range(2)]
+
+        def sum_pair(bank, first, g):
+            for b in range(4):
+                turn(blk(bank, b), blk(g, b), first and b == 0, (not first) and b == 3)
+
+        def step_g1(t):
+            fetch(g1[t], ywin[t], "n1")
+            sum_pair(s1_bank, True, g1[t])
+
+        def step_g3(t):
+            fetch(g3[t], dwin[t], "n3")
+            sum_pair(s1_bank, False, g3[t])
+            nc.scalar.copy(s1t[t][:], s1_bank[:])
+
+        def step_g2(t):
+            fetch(g2[t], ywin[t], "n2")
+            sum_pair(s2_bank, True, g2[t])
+
+        def step_g4(t):
+            fetch(g4[t], dwin[t], "n4")
+            sum_pair(s2_bank, False, g4[t])
+
+        def into_pair(bank2, src, t, a, start, stop):
+            e = t % 2
+            for jb in range(2):
+                turn(blk(bank2[a], 2 * jb + e), blk(src, 2 * a + jb), start and jb == 0, stop and jb == 1)
+
+        def step_max(t):
+            nc.vector.tensor_tensor(m1t[t][:], s2_bank[:], s1t[t][:], ALU.max)
+            bank = mm_bank[t % 2]
+            for b in range(4):
+                turn(blk(bank, b), blk(m1t[t], b), True, True)
+            nc.scalar.activation(ywin[t][:, :S], bank[:], ACT.Copy, scale=gain[:, t : t + 1])
+
+        def step_g5(t, halves):
+            for a in range(2):
+                into_pair(num_bank, ywin[t], t, a, t % 2 == 0, False)
+            for lo, hi in halves:
+                nc.vector.tensor_scalar(g5[t][:, lo:hi], ywin[t][:].indirect(lists["n5"][:, lo // 16 : hi // 16]), -1.0, 0.0, ALU.mult, ALU.add)
+                for a in range(lo // HALF, hi // HALF):
+                    into_pair(num_bank, g5[t], t, a, False, t % 2 == 1)
+
+        def step_g6(t):
+            for a in range(2):
+                into_pair(den_bank, bwin[t], t, a, t % 2 == 0, False)
+            fetch(g6[t], bwin[t], "n6")
+            for a in range(2):
+                into_pair(den_bank, g6[t], t, a, False, t % 2 == 1)
+            if t % 2 == 1:
+                u = t // 2
+                for a in range(2):
+                    nc.scalar.activation(rs[u][a][:].rearrange("p (b m e) -> p b m e", b=2, e=2),
+                                         den_bank[a][:].rearrange("p (b e m) -> p b m e", b=2, e=2),
+                                         ACT.Abs_reciprocal_sqrt, bias=0.5)
+                    nc.scalar.activation(rt[u][a][:], rs[u][a][:], ACT.Square)
+
+        def step_mult(u, a):
+            nc.vector.tensor_tensor(zt[u][a][:].rearrange("p (b m e) -> p b m e", b=2, e=2),
+                                    num_bank[a][:].rearrange("p (b e m) -> p b m e", b=2, e=2),
+                                    rt[u][a][:].rearrange("p (b m e) -> p b m e", b=2, e=2), ALU.mult)
+
+        word_bank = [s1_bank, s2_bank]
+
+        def step_words(u, a):
+            words = zt[u][a][:].bitcast(F32)
+            for jb in range(2):
+                turn(blk(word_bank[a], 2 * u + jb), blk(words, jb), True, True)
+
+        whole = [(0, S)]
+        halves = [(0, HALF), (HALF, S)]
+
+        step_g1(0)
+        step_g2(0)
+        step_g3(0)
+        weave("w3")
+        step_g4(0)
+        step_g1(1)
+        step_max(0)
+        quant_w("w3")
+        for t in range(PACK):
+            product(den_bank[t % 2][:], "w3", t, xcode["three"][:], xscale["three"][:])
+            nc.scalar.activation(bwin[t][:, :S], den_bank[t % 2][:], ACT.Abs)
+        step_g3(1)
+        step_g2(1)
+        step_g4(1)
+        step_g5(0, whole)
+        step_g1(2)
+        step_max(1)
+        step_g3(2)
+        step_g6(0)
+        step_g2(2)
+        step_g4(2)
+        weave("w4")
+        step_g6(1)
+        step_g5(1, whole)
+        step_g1(3)
+        step_max(2)
+        step_g3(3)
+        step_mult(0, 0)
+        step_mult(0, 1)
+        step_g2(3)
+        step_g4(3)
+        step_g6(2)
+        step_max(3)
+        step_words(0, 0)
+        step_words(0, 1)
+        step_g6(3)
+        step_g5(2, whole)
+        step_g5(3, halves)
+
+        zin = [sb("zin%d" % a, [P, PACK * HALF], BF16) for a in range(2)]
+        zcode = [sb("zc%d" % a, [P, HALF], U32) for a in range(2)]
+        zscale = [sb("zs%d" % a, [P, HALF], U8) for a in range(2)]
+        for a in range(2):
+            step_mult(1, a)
+            step_words(1, a)
+            nc.scalar.copy(zin[a][:].bitcast(F32).rearrange("p (j u) -> p j u", u=2), word_bank[a][:].rearrange("p (u j) -> p j u", u=2))
+        quant_w("w4", "rt_1_0")
+        h_bank = [banks[0], banks[1], banks[6], banks[7]]
+        hwin = dwin
+        for a in range(2):
+            nc.vector.quantize_mx(out=zcode[a][:].bitcast(FP8X4), scales=zscale[a][:], in_=zin[a][:])
+            product(h_bank[0][:, HALF * a : HALF * (a + 1)], "w4", 0, zcode[a][:], zscale[a][:])
+            nc.scalar.copy(hwin[0][:, HALF * a : HALF * (a + 1)], h_bank[0][:, HALF * a : HALF * (a + 1)])
+        for t in range(1, PACK):
+            for a in range(2):
+                product(h_bank[t][:, HALF * a : HALF * (a + 1)], "w4", t, zcode[a][:], zscale[a][:])
+            nc.scalar.copy(hwin[t][:, :S], h_bank[t][:])
+
+        out_rows = out.rearrange("(p t) j -> p t j", t=PACK)
+        pieces = [(0, 0, S), (1, 0, S), (2, 0, S), (3, 0, HALF), (3, HALF, S)]
+
+        def fetch_h(dst, t, lname, lo, hi):
+            if t < 3:
+                nc.vector.tensor_scalar(dst[:, lo:hi], hwin[t][:].indirect(lists[lname][:, lo // 16 : hi // 16]), -4.0 / 3.0, 0.0, ALU.mult, ALU.add)
+            else:
+                fetch(dst, hwin[t], lname, lo, hi)
+
+        def step_hmax(t, lo, hi):
+            nc.vector.tensor_tensor(g3[t][:, lo:hi], g1[t][:, lo:hi], g2[t][:, lo:hi], ALU.min if t < 3 else ALU.max)
+
+        def step_out(t, lo, hi):
+            if t < 3:
+                across, back = banks[4 + t % 2], banks[2 + t % 2]
+                sum_pair(across, True, hwin[t])
+                sum_pair(across, False, g3[t])
+                nc.scalar.activation(g5[t][:], across[:], ACT.Copy, scale=-0.75)
+                for b in range(4):
+                    turn(blk(back, b), blk(g5[t], b), True, True)
+                nc.scalar.copy(g4[t][:], back[:])
+            else:
+                nc.vector.scalar_tensor_tensor(g4[t][:, lo:hi], h_bank[t][:, lo:hi], -0.75, g3[t][:, lo:hi], ALU.mult, ALU.add)
+            nc.sync.dma_start(out_rows[:, t, lo:hi], g4[t][:, lo:hi])
+
+        for i, (t, lo, hi) in enumerate(pieces):
+            fetch_h(g1[t], t, "n7", lo, hi)
+            if i > 0:
+                step_hmax(*pieces[i - 1])
+            fetch_h(g2[t], t, "n8", lo, hi)
+            if i > 0:
+                step_out(*pieces[i - 1])
+        step_hmax(*pieces[-1])
+        step_out(*pieces[-1])

@@ -4,7 +4,7 @@ import concourse.mybir as mybir
 from concourse.masks import make_identity
 
 K, T, S, N, H = 512, 2048, 512, 512, 512
-FLOPS = 4 * 2 * 512 * 512 * 512
+FLOPS = 2 * S * (3 * K * H + H * N)
 
 F32 = mybir.dt.float32
 BF16 = mybir.dt.bfloat16
@@ -18,303 +18,375 @@ ACT = mybir.ActivationFunctionType
 
 P = 128
 PACK = 4
+BLOCKS = S // P
 HALF = S // 2
-COLS = S // 16
+LAST = PACK - 1
+RING = 5
+HALVES = ((0, HALF), (HALF, S))
+Z_PIECES = ((0, HALF), (HALF, HALF + P), (HALF + P, S))
 
 
-def tile_picked_triopathbnormbover_none_p_kernel(tc, x_words, x_scales, w1, w2, w3, gn, w4, offs, two, three, n1, n2, n3, n4, n5, n6, n7, n8, out):
+def tile_picked_triopathbnormbover_none_p_kernel(
+    tc, x_words, x_scales, w1, w2, w3, gn, w4, offs, two, three, n1, n2, n3, n4, n5, n6, n7, n8, out
+):
     nc = tc.nc
     with ExitStack() as ctx:
         keep = ctx.enter_context(tc.tile_pool(name="keep", bufs=1))
         psum = ctx.enter_context(tc.psum_pool(name="psum", bufs=1))
 
-        def sb(name, shape, dtype, tag=None):
-            return keep.tile(shape, dtype, name=name, tag=tag or name, align_bytes=64)
+        def sbuf(name, shape, dtype, on=None):
+            return keep.tile(shape, dtype, name=name, tag=on or name, align_bytes=64)
+
+        def tiles(name, width):
+            return [sbuf("%s%d" % (name, t), [P, width], F32) for t in range(PACK)]
 
         banks = [psum.tile([P, S], F32, name="bank%d" % i) for i in range(8)]
-        mm_bank = banks[0:2]
-        s1_bank, s2_bank = banks[2], banks[3]
-        num_bank = banks[4:6]
-        den_bank = banks[6:8]
 
-        lists = {}
+        lists, raw = {}, {}
 
         def load_list(name, ap):
-            lists[name] = sb("list_" + name, [P, COLS], U16)
+            lists[name] = sbuf("list_" + name, [P, S // 16], U16)
             nc.sync.dma_start(lists[name][:], ap)
 
-        raw = {}
-
-        def load_w(name, ap, parts):
+        def load_weight(name, ap, parts):
             width = H // parts
-            raw[name] = [sb("raw_%s_%d" % (name, i), [P, PACK, width], F32) for i in range(parts)]
+            raw[name] = [sbuf("raw_%s_%d" % (name, i), [P, PACK, width], F32) for i in range(parts)]
             for i in range(parts):
                 nc.sync.dma_start(raw[name][i][:], ap.rearrange("(p j) c -> p j c", j=PACK)[:, :, width * i : width * (i + 1)])
 
-        xs = sb("xs", [P, T], U8)
-        nc.gpsimd.memset(xs[:].bitcast(I32), 0)
+        scale_table = sbuf("scale_table", [P, T], U8)
+        nc.gpsimd.memset(scale_table[:].bitcast(I32), 0)
+        for q in range(4):
+            nc.sync.dma_start(scale_table[32 * q : 32 * q + 4, :].bitcast(I32), x_scales[0, 4 * q : 4 * q + 4, :].bitcast(I32))
         load_list("offs", offs)
         load_list("two", two)
         load_list("three", three)
-        xw = sb("xw", [P, T], I32)
-        nc.sync.dma_start(xw[:], x_words[0].rearrange("p n t -> p (n t)").bitcast(I32))
-        for q in range(4):
-            nc.scalar.dma_start(xs[32 * q : 32 * q + 4, :].bitcast(I32), x_scales[0, 4 * q : 4 * q + 4, :].bitcast(I32))
-        load_w("w1", w1, 2)
-        load_w("w2", w2, 1)
+        word_table = sbuf("word_table", [P, T], I32)
+        nc.sync.dma_start(word_table[:], x_words[0].rearrange("p n t -> p (n t)").bitcast(I32))
+        load_weight("w1", w1, 2)
+        load_weight("w2", w2, 1)
         load_list("n1", n1)
         load_list("n2", n2)
         load_list("n3", n3)
         load_list("n4", n4)
-        load_w("w3", w3, 1)
-        gain = sb("gain", [P, PACK], F32)
+        load_weight("w3", w3, 1)
+        gain = sbuf("gain", [P, PACK], F32)
         nc.sync.dma_start(gain[:], gn.rearrange("(p t) o -> p (t o)", t=PACK))
         load_list("n6", n6)
         load_list("n5", n5)
-        load_w("w4", w4, 1)
+        load_weight("w4", w4, 1)
         load_list("n7", n7)
         load_list("n8", n8)
 
-        ident = sb("ident", [P, P], F32)
+        four = sbuf("four", [P, 1], F32)
+        one_half = sbuf("one_half", [P, 1], F32)
+        nc.gpsimd.memset(four[:], 4.0)
+        nc.scalar.activation(one_half[:], four[:], ACT.Abs_reciprocal_sqrt)
+
+        ident = sbuf("ident", [P, P], F32)
         make_identity(nc, ident[:])
 
-        warm = sb("warm", [P, 2], F32)
-        nc.vector.memset(warm[:, 0:1], 1.0)
-        nc.scalar.activation(warm[:, 1:2], warm[:, 0:1], ACT.Abs_reciprocal_sqrt)
+        y_win, d_win, b_win = tiles("y_win", 2 * S), tiles("d_win", 2 * S), tiles("b_win", 2 * S)
+        m_win = y_win[:LAST] + [sbuf("m_win_last", [P, S], F32)]
+        h_win = d_win
 
-        ywin = [sb("ywin%d" % t, [P, 2 * S], F32) for t in range(PACK)]
-        dwin = [sb("dwin%d" % t, [P, 2 * S], F32) for t in range(PACK)]
-        bwin = [sb("bwin%d" % t, [P, 2 * S], F32) for t in range(PACK)]
+        x_code, x_scale, dealt, w_code, w_scale = {}, {}, {}, {}, {}
 
-        xcode, xscale = {}, {}
+        def pick_words(name, on=None):
+            x_code[name] = sbuf("x_code_" + name, [P, S], U32, on)
+            nc.vector.tensor_copy(x_code[name][:], word_table[:].bitcast(U32).indirect(lists[name][:]))
 
-        def pick_words(name, tag=None):
-            xcode[name] = sb("xc_" + name, [P, S], U32, tag)
-            nc.vector.tensor_copy(xcode[name][:], xw[:].bitcast(U32).indirect(lists[name][:]))
+        def pick_scales(name):
+            x_scale[name] = sbuf("x_scale_" + name, [P, S], U8)
+            nc.vector.tensor_copy(x_scale[name][:], scale_table[:].indirect(lists[name][:]))
 
-        def pick_bytes(name):
-            xscale[name] = sb("xb_" + name, [P, S], U8)
-            nc.vector.tensor_copy(xscale[name][:], xs[:].indirect(lists[name][:]))
+        def deal(name, step):
+            dealt[name] = sbuf("dealt_" + name, [P, PACK * H], BF16)
+            dst = dealt[name][:].rearrange("p (t m j) -> p m j t", t=PACK, j=PACK)
+            per_part = P // len(raw[name])
+            for m in range(0, P, step):
+                src = raw[name][m // per_part][:].rearrange("p j (m t) -> p m j t", t=PACK)
+                nc.scalar.copy(dst[:, m : m + step], src[:, m % per_part : m % per_part + step])
 
-        grouped, wcode, wscale = {}, {}, {}
+        def quantise_weight(name, on=None):
+            w_code[name] = sbuf("w_code_" + name, [P, H], U32, on)
+            w_scale[name] = sbuf("w_scale_" + name, [P, H], U8)
+            nc.vector.quantize_mx(out=w_code[name][:].bitcast(FP8X4), scales=w_scale[name][:], in_=dealt[name][:])
 
-        def weave(name):
-            grouped[name] = sb("grp_" + name, [P, PACK * H], BF16)
-            dst = grouped[name][:].rearrange("p (t m j) -> p m j t", t=PACK, j=PACK)
-            for i in range(2):
-                if len(raw[name]) == 2:
-                    src = raw[name][i][:].rearrange("p j (m t) -> p m j t", t=PACK)
-                else:
-                    src = raw[name][0][:].rearrange("p j (m t) -> p m j t", t=PACK)[:, 64 * i : 64 * (i + 1)]
-                nc.scalar.copy(dst[:, 64 * i : 64 * (i + 1)], src)
+        def block(ap, b):
+            return ap[:, P * b : P * (b + 1)]
 
-        def quant_w(name, tag=None):
-            wcode[name] = sb("wc_" + name, [P, H], U32, tag)
-            wscale[name] = sb("ws_" + name, [P, H], U8)
-            nc.vector.quantize_mx(out=wcode[name][:].bitcast(FP8X4), scales=wscale[name][:], in_=grouped[name][:])
+        def product(dst, w_name, t, codes, scales):
+            nc.tensor.matmul_mx(
+                out=dst,
+                lhsT=block(w_code[w_name], t).bitcast(FP8X4),
+                lhsT_scale=block(w_scale[w_name], t),
+                rhs=codes.bitcast(FP8X4),
+                rhs_scale=scales,
+                start=True,
+                stop=True,
+            )
 
-        def product(bank_ap, wname, t, codes, scales):
-            cols = slice(P * t, P * (t + 1))
-            nc.tensor.matmul_mx(out=bank_ap, lhsT=wcode[wname][:, cols].bitcast(FP8X4), lhsT_scale=wscale[wname][:, cols],
-                                rhs=codes.bitcast(FP8X4), rhs_scale=scales, start=True, stop=True)
+        def make_y(t, bank):
+            product(bank[:], "w1", t, x_code["offs"][:], x_scale["offs"][:])
+            nc.scalar.copy(y_win[t][:, :S], bank[:])
+
+        def make_d(t, bank):
+            product(bank[:], "w2", t, x_code["two"][:], x_scale["two"][:])
+            nc.scalar.copy(d_win[t][:, :S], bank[:])
+
+        def make_abs_b(t, bank):
+            product(bank[:], "w3", t, x_code["three"][:], x_scale["three"][:])
+            nc.scalar.activation(b_win[t][:, :S], bank[:], ACT.Abs)
+
+        def fetch(dst, win, list_name, lo=0, hi=S):
+            nc.vector.tensor_copy(dst[:, lo:hi], win[:].indirect(lists[list_name][:, lo // 16 : hi // 16]))
+
+        def fetch_times(dst, win, list_name, factor, lo=0, hi=S):
+            offsets = lists[list_name][:, lo // 16 : hi // 16]
+            nc.vector.tensor_scalar(dst[:, lo:hi], win[:].indirect(offsets), factor, 0.0, ALU.mult, ALU.add)
 
         def turn(dst, src, start, stop):
             nc.tensor.matmul(dst, lhsT=src, rhs=ident[:], start=start, stop=stop, is_transpose=True)
 
-        def blk(ap, b):
-            return ap[:, P * b : P * (b + 1)]
+        def add_turned(bank, src, opens, closes):
+            for b in range(BLOCKS):
+                turn(block(bank, b), block(src, b), opens and b == 0, closes and b == BLOCKS - 1)
 
-        def fetch(name, win, lname, lo=0, hi=S):
-            nc.vector.tensor_copy(name[:, lo:hi], win[:].indirect(lists[lname][:, lo // 16 : hi // 16]))
+        ring = [sbuf("ring%d" % i, [P, S], F32) for i in range(RING)]
+        handed_out = []
 
-        pick_bytes("offs")
-        pick_bytes("two")
-        pick_bytes("three")
-        pick_words("offs")
-        pick_words("two")
-        weave("w1")
-        quant_w("w1")
-        pick_words("three", "raw_w1_1")
-        for t in range(PACK):
-            product(mm_bank[t % 2][:], "w1", t, xcode["offs"][:], xscale["offs"][:])
-            nc.scalar.copy(ywin[t][:, :S], mm_bank[t % 2][:])
-        weave("w2")
-        quant_w("w2")
-        for t in range(PACK):
-            product(mm_bank[t % 2][:], "w2", t, xcode["two"][:], xscale["two"][:])
-            nc.scalar.copy(dwin[t][:, :S], mm_bank[t % 2][:])
+        def next_in_ring():
+            handed_out.append(ring[len(handed_out) % RING])
+            return handed_out[-1]
 
-        g1 = [sb("g1_%d" % t, [P, S], F32) for t in range(PACK)]
-        g2 = [sb("g2_%d" % t, [P, S], F32) for t in range(PACK)]
-        g3 = [sb("g3_%d" % t, [P, S], F32) for t in range(PACK)]
-        g4 = [sb("g4_%d" % t, [P, S], F32) for t in range(PACK)]
-        g5 = [sb("g5_%d" % t, [P, S], F32) for t in range(PACK)]
-        g6 = [sb("g6_%d" % t, [P, S], F32) for t in range(PACK)]
-        s1t = [sb("s1t_%d" % t, [P, S], F32) for t in range(PACK)]
-        m1t = [sb("m1t_%d" % t, [P, S], F32) for t in range(PACK)]
-        rt = [[sb("rt_%d_%d" % (u, a), [P, S], F32) for a in range(2)] for u in range(2)]
-        rs = [[sb("rs_%d_%d" % (u, a), [P, S], F32) for a in range(2)] for u in range(2)]
-        zt = [[sb("zt_%d_%d" % (u, a), [P, S], BF16) for a in range(2)] for u in range(2)]
+        m_bank, neg_bank, diff_bank = banks[0], banks[2], banks[3]
+        base = tiles("base", S)
+        rise = [sbuf("rise%d" % t, [P, S], F32) for t in range(LAST)]
+        rise_blocks = [[block(rise[t], b) for b in range(BLOCKS)] for t in range(LAST)]
+        rise_last = [y_win[1 + a][:, S : S + HALF] for a in range(2)]
+        rise_blocks.append([block(rise_last[b // 2], b % 2) for b in range(BLOCKS)])
 
-        def sum_pair(bank, first, g):
-            for b in range(4):
-                turn(blk(bank, b), blk(g, b), first and b == 0, (not first) and b == 3)
+        def look_up_n1(t):
+            g = next_in_ring()
+            fetch_times(g, y_win[t], "n1", -1.0)
+            add_turned(neg_bank, g, True, False)
+            add_turned(diff_bank, g, True, False)
 
-        def step_g1(t):
-            fetch(g1[t], ywin[t], "n1")
-            sum_pair(s1_bank, True, g1[t])
+        def look_up_n3(t):
+            g = next_in_ring()
+            fetch_times(g, d_win[t], "n3", -1.0)
+            add_turned(neg_bank, g, False, True)
+            add_turned(diff_bank, g, False, False)
+            nc.scalar.activation(base[t][:], neg_bank[:], ACT.Copy, scale=-1.0)
 
-        def step_g3(t):
-            fetch(g3[t], dwin[t], "n3")
-            sum_pair(s1_bank, False, g3[t])
-            nc.scalar.copy(s1t[t][:], s1_bank[:])
+        def look_up_n2(t):
+            g = next_in_ring()
+            fetch(g, y_win[t], "n2")
+            add_turned(diff_bank, g, False, False)
 
-        def step_g2(t):
-            fetch(g2[t], ywin[t], "n2")
-            sum_pair(s2_bank, True, g2[t])
+        def look_up_n4(t):
+            g = next_in_ring()
+            fetch(g, d_win[t], "n4")
+            add_turned(diff_bank, g, False, True)
+            if t < LAST:
+                nc.scalar.activation(rise[t][:], diff_bank[:], ACT.Relu)
+            else:
+                for a, (lo, hi) in enumerate(HALVES):
+                    nc.scalar.activation(rise_last[a], diff_bank[:, lo:hi], ACT.Relu)
 
-        def step_g4(t):
-            fetch(g4[t], dwin[t], "n4")
-            sum_pair(s2_bank, False, g4[t])
+        def make_gained_m1(t):
+            add_turned(m_bank, base[t], True, False)
+            for b in range(BLOCKS):
+                turn(block(m_bank, b), rise_blocks[t][b], False, b == BLOCKS - 1)
+            nc.scalar.activation(m_win[t][:, :S], m_bank[:], ACT.Copy, scale=gain[:, t : t + 1])
 
-        def into_pair(bank2, src, t, a, start, stop):
-            e = t % 2
-            for jb in range(2):
-                turn(blk(bank2[a], 2 * jb + e), blk(src, 2 * a + jb), start and jb == 0, stop and jb == 1)
+        pieces = (HALVES, Z_PIECES)
+        num_bank = (banks[4:6], banks[1:4])
+        den_bank = banks[6:8]
+        unit_bank = banks[4:7]
+        root = [[sbuf("root_%d_%d" % (u, a), [P, S], F32) for a in range(2)] for u in range(2)]
+        inverse = [[sbuf("inverse_%d_%d" % (u, a), [P, S], F32) for a in range(2)] for u in range(2)]
+        z_turned = [[sbuf("z_turned_%d_%d" % (u, i), [P, 2 * (hi - lo)], BF16) for i, (lo, hi) in enumerate(pieces[u])] for u in range(2)]
 
-        def step_max(t):
-            nc.vector.tensor_tensor(m1t[t][:], s2_bank[:], s1t[t][:], ALU.max)
-            bank = mm_bank[t % 2]
-            for b in range(4):
-                turn(blk(bank, b), blk(m1t[t], b), True, True)
-            nc.scalar.activation(ywin[t][:, :S], bank[:], ACT.Copy, scale=gain[:, t : t + 1])
+        def add_to_pair(bank, src, t, lo, hi, opens, closes):
+            first, end = lo // P, hi // P
+            for b in range(first, end):
+                turn(block(bank, 2 * (b - first) + t % 2), block(src, b), opens and b == first, closes and b == end - 1)
 
-        def step_g5(t, halves):
-            for a in range(2):
-                into_pair(num_bank, ywin[t], t, a, t % 2 == 0, False)
-            for lo, hi in halves:
-                nc.vector.tensor_scalar(g5[t][:, lo:hi], ywin[t][:].indirect(lists["n5"][:, lo // 16 : hi // 16]), -1.0, 0.0, ALU.mult, ALU.add)
-                for a in range(lo // HALF, hi // HALF):
-                    into_pair(num_bank, g5[t], t, a, False, t % 2 == 1)
+        def look_up_n5(t):
+            u = t // 2
+            for i, (lo, hi) in enumerate(pieces[u]):
+                add_to_pair(num_bank[u][i], m_win[t], t, lo, hi, t % 2 == 0, False)
+            g = next_in_ring()
+            if t < LAST:
+                fetch_times(g, m_win[t], "n5", -1.0)
+            for i, (lo, hi) in enumerate(pieces[u]):
+                if t == LAST:
+                    fetch_times(g, m_win[t], "n5", -1.0, lo, hi)
+                add_to_pair(num_bank[u][i], g, t, lo, hi, False, t % 2 == 1)
 
-        def step_g6(t):
-            for a in range(2):
-                into_pair(den_bank, bwin[t], t, a, t % 2 == 0, False)
-            fetch(g6[t], bwin[t], "n6")
-            for a in range(2):
-                into_pair(den_bank, g6[t], t, a, False, t % 2 == 1)
+        def look_up_n6(t):
+            for a, (lo, hi) in enumerate(HALVES):
+                add_to_pair(den_bank[a], b_win[t], t, lo, hi, t % 2 == 0, False)
+            g = next_in_ring()
+            fetch(g, b_win[t], "n6")
+            for a, (lo, hi) in enumerate(HALVES):
+                add_to_pair(den_bank[a], g, t, lo, hi, False, t % 2 == 1)
             if t % 2 == 1:
                 u = t // 2
                 for a in range(2):
-                    nc.scalar.activation(rs[u][a][:].rearrange("p (b m e) -> p b m e", b=2, e=2),
-                                         den_bank[a][:].rearrange("p (b e m) -> p b m e", b=2, e=2),
-                                         ACT.Abs_reciprocal_sqrt, bias=0.5)
-                    nc.scalar.activation(rt[u][a][:], rs[u][a][:], ACT.Square)
+                    nc.scalar.activation(
+                        root[u][a][:].rearrange("j (b p e) -> j b p e", b=2, e=2),
+                        den_bank[a][:].rearrange("j (b e p) -> j b p e", b=2, e=2),
+                        ACT.Abs_reciprocal_sqrt,
+                        bias=one_half[:],
+                    )
+                    nc.scalar.activation(inverse[u][a][:], root[u][a][:], ACT.Square)
 
-        def step_mult(u, a):
-            nc.vector.tensor_tensor(zt[u][a][:].rearrange("p (b m e) -> p b m e", b=2, e=2),
-                                    num_bank[a][:].rearrange("p (b e m) -> p b m e", b=2, e=2),
-                                    rt[u][a][:].rearrange("p (b m e) -> p b m e", b=2, e=2), ALU.mult)
+        def form_z(u, i):
+            lo, hi = pieces[u][i]
+            count, first = 2 * (hi - lo), 2 * (lo % HALF)
+            nc.vector.tensor_tensor(
+                z_turned[u][i][:].rearrange("j (b p e) -> j b p e", p=P, e=2),
+                num_bank[u][i][:, :count].rearrange("j (b e p) -> j b p e", p=P, e=2),
+                inverse[u][lo // HALF][:, first : first + count].rearrange("j (b p e) -> j b p e", p=P, e=2),
+                ALU.mult,
+            )
 
-        word_bank = [s1_bank, s2_bank]
+        def turn_z_back(u, i):
+            lo, hi = pieces[u][i]
+            units = z_turned[u][i][:].bitcast(F32)
+            for b in range(lo // P, hi // P):
+                k = [z_lo <= P * b < z_hi for z_lo, z_hi in Z_PIECES].index(True)
+                z_lo, z_hi = Z_PIECES[k]
+                turn(block(unit_bank[k], u * ((z_hi - z_lo) // P) + b - z_lo // P), block(units, b - lo // P), True, True)
 
-        def step_words(u, a):
-            words = zt[u][a][:].bitcast(F32)
-            for jb in range(2):
-                turn(blk(word_bank[a], 2 * u + jb), blk(words, jb), True, True)
+        for name in ("offs", "two", "three"):
+            pick_scales(name)
+        pick_words("offs")
+        pick_words("two")
+        deal("w1", P // 2)
+        quantise_weight("w1")
+        pick_words("three", on="raw_w1_1")
 
-        whole = [(0, S)]
-        halves = [(0, HALF), (HALF, S)]
+        make_y(0, banks[0])
+        deal("w2", P // 4)
+        look_up_n1(0)
+        quantise_weight("w2")
+        make_d(0, banks[1])
+        make_y(1, banks[4])
+        look_up_n2(0)
+        look_up_n3(0)
+        make_d(1, banks[7])
+        look_up_n4(0)
+        deal("w3", P // 2)
+        make_y(2, banks[5])
+        make_d(2, banks[0])
+        look_up_n1(1)
+        make_gained_m1(0)
+        look_up_n3(1)
+        quantise_weight("w3")
+        make_abs_b(0, banks[1])
+        make_y(3, banks[6])
+        make_d(3, banks[4])
+        make_abs_b(1, banks[7])
+        look_up_n2(1)
+        look_up_n4(1)
+        make_abs_b(2, banks[5])
+        make_abs_b(3, banks[1])
+        look_up_n6(0)
+        make_gained_m1(1)
 
-        step_g1(0)
-        step_g2(0)
-        step_g3(0)
-        weave("w3")
-        step_g4(0)
-        step_g1(1)
-        step_max(0)
-        quant_w("w3")
-        for t in range(PACK):
-            product(den_bank[t % 2][:], "w3", t, xcode["three"][:], xscale["three"][:])
-            nc.scalar.activation(bwin[t][:, :S], den_bank[t % 2][:], ACT.Abs)
-        step_g3(1)
-        step_g2(1)
-        step_g4(1)
-        step_g5(0, whole)
-        step_g1(2)
-        step_max(1)
-        step_g3(2)
-        step_g6(0)
-        step_g2(2)
-        step_g4(2)
-        weave("w4")
-        step_g6(1)
-        step_g5(1, whole)
-        step_g1(3)
-        step_max(2)
-        step_g3(3)
-        step_mult(0, 0)
-        step_mult(0, 1)
-        step_g2(3)
-        step_g4(3)
-        step_g6(2)
-        step_max(3)
-        step_words(0, 0)
-        step_words(0, 1)
-        step_g6(3)
-        step_g5(2, whole)
-        step_g5(3, halves)
+        look_up_n1(2)
+        look_up_n3(2)
+        look_up_n5(0)
+        look_up_n2(2)
+        look_up_n4(2)
+        look_up_n6(1)
+        make_gained_m1(2)
+        look_up_n1(3)
+        deal("w4", P // 2)
+        look_up_n3(3)
+        look_up_n2(3)
+        look_up_n4(3)
+        look_up_n6(2)
+        make_gained_m1(3)
 
-        zin = [sb("zin%d" % a, [P, PACK * HALF], BF16) for a in range(2)]
-        zcode = [sb("zc%d" % a, [P, HALF], U32) for a in range(2)]
-        zscale = [sb("zs%d" % a, [P, HALF], U8) for a in range(2)]
-        for a in range(2):
-            step_mult(1, a)
-            step_words(1, a)
-            nc.scalar.copy(zin[a][:].bitcast(F32).rearrange("p (j u) -> p j u", u=2), word_bank[a][:].rearrange("p (u j) -> p j u", u=2))
-        quant_w("w4", "rt_1_0")
-        h_bank = [banks[0], banks[1], banks[6], banks[7]]
-        hwin = dwin
-        for a in range(2):
-            nc.vector.quantize_mx(out=zcode[a][:].bitcast(FP8X4), scales=zscale[a][:], in_=zin[a][:])
-            product(h_bank[0][:, HALF * a : HALF * (a + 1)], "w4", 0, zcode[a][:], zscale[a][:])
-            nc.scalar.copy(hwin[0][:, HALF * a : HALF * (a + 1)], h_bank[0][:, HALF * a : HALF * (a + 1)])
+        look_up_n6(3)
         for t in range(1, PACK):
-            for a in range(2):
-                product(h_bank[t][:, HALF * a : HALF * (a + 1)], "w4", t, zcode[a][:], zscale[a][:])
-            nc.scalar.copy(hwin[t][:, :S], h_bank[t][:])
+            look_up_n5(t)
+        for a in range(2):
+            form_z(0, a)
+        for a in range(2):
+            turn_z_back(0, a)
+
+        z_rows = [sbuf("z_rows%d" % i, [P, PACK * (hi - lo)], BF16) for i, (lo, hi) in enumerate(Z_PIECES)]
+        z_code = sbuf("z_code", [P, S], U32)
+        z_scale = sbuf("z_scale", [P, S], U8)
+        for i, (lo, hi) in enumerate(Z_PIECES):
+            form_z(1, i)
+            turn_z_back(1, i)
+            nc.scalar.copy(
+                z_rows[i][:].bitcast(F32).rearrange("p (j u) -> p j u", u=2),
+                unit_bank[i][:, : 2 * (hi - lo)].rearrange("p (u j) -> p j u", u=2),
+            )
+        quantise_weight("w4", on="inverse_1_1")
+
+        h_first_bank = [banks[0], banks[7], banks[1]]
+        for i, (lo, hi) in enumerate(Z_PIECES):
+            nc.vector.quantize_mx(out=z_code[:, lo:hi].bitcast(FP8X4), scales=z_scale[:, lo:hi], in_=z_rows[i][:])
+            product(h_first_bank[i][:, : hi - lo], "w4", 0, z_code[:, lo:hi], z_scale[:, lo:hi])
+            nc.scalar.copy(h_win[0][:, lo:hi], h_first_bank[i][:, : hi - lo])
+        for t in range(1, PACK):
+            product(banks[1 + t][:], "w4", t, z_code[:], z_scale[:])
+            nc.scalar.copy(h_win[t][:, :S], banks[1 + t][:])
+        h_last_bank = banks[1 + LAST]
 
         out_rows = out.rearrange("(p t) j -> p t j", t=PACK)
-        pieces = [(0, 0, S), (1, 0, S), (2, 0, S), (3, 0, HALF), (3, HALF, S)]
+        low_bank = [banks[0], banks[1], banks[3]]
+        gap_bank = [banks[7], banks[2], banks[7]]
+        out_bank = [banks[5], banks[6], banks[5]]
+        top, result = tiles("top", S), tiles("result", S)
 
-        def fetch_h(dst, t, lname, lo, hi):
-            if t < 3:
-                nc.vector.tensor_scalar(dst[:, lo:hi], hwin[t][:].indirect(lists[lname][:, lo // 16 : hi // 16]), -4.0 / 3.0, 0.0, ALU.mult, ALU.add)
-            else:
-                fetch(dst, hwin[t], lname, lo, hi)
+        def finish_turned(t):
+            add_turned(out_bank[t], top[t], False, True)
+            nc.scalar.copy(result[t][:], out_bank[t][:])
+            nc.scalar.dma_start(out_rows[:, t, :], result[t][:])
 
-        def step_hmax(t, lo, hi):
-            nc.vector.tensor_tensor(g3[t][:, lo:hi], g1[t][:, lo:hi], g2[t][:, lo:hi], ALU.min if t < 3 else ALU.max)
+        for t in range(LAST):
+            at_n7 = sbuf("at_n7_%d" % t, [P, S], F32)
+            fetch_times(at_n7, h_win[t], "n7", -4.0 / 3.0)
+            add_turned(low_bank[t], h_win[t], True, False)
+            add_turned(low_bank[t], at_n7, False, True)
+            add_turned(gap_bank[t], at_n7, True, False)
+            nc.scalar.activation(base[t][:], low_bank[t][:], ACT.Copy, scale=-0.75)
+            add_turned(out_bank[t], base[t], True, False)
+            at_n8 = sbuf("at_n8_%d" % t, [P, S], F32)
+            fetch_times(at_n8, h_win[t], "n8", 4.0 / 3.0)
+            add_turned(gap_bank[t], at_n8, False, True)
+            nc.scalar.activation(top[t][:], gap_bank[t][:], ACT.Relu, scale=0.75)
+            if t > 0:
+                finish_turned(t - 1)
+        finish_turned(LAST - 1)
 
-        def step_out(t, lo, hi):
-            if t < 3:
-                across, back = banks[4 + t % 2], banks[2 + t % 2]
-                sum_pair(across, True, hwin[t])
-                sum_pair(across, False, g3[t])
-                nc.scalar.activation(g5[t][:], across[:], ACT.Copy, scale=-0.75)
-                for b in range(4):
-                    turn(blk(back, b), blk(g5[t], b), True, True)
-                nc.scalar.copy(g4[t][:], back[:])
-            else:
-                nc.vector.scalar_tensor_tensor(g4[t][:, lo:hi], h_bank[t][:, lo:hi], -0.75, g3[t][:, lo:hi], ALU.mult, ALU.add)
-            nc.sync.dma_start(out_rows[:, t, lo:hi], g4[t][:, lo:hi])
+        last_n7 = [sbuf("last_n7_%d" % a, [P, S], F32) for a in range(2)]
+        last_n8 = [sbuf("last_n8_%d" % a, [P, S], F32) for a in range(2)]
 
-        for i, (t, lo, hi) in enumerate(pieces):
-            fetch_h(g1[t], t, "n7", lo, hi)
-            if i > 0:
-                step_hmax(*pieces[i - 1])
-            fetch_h(g2[t], t, "n8", lo, hi)
-            if i > 0:
-                step_out(*pieces[i - 1])
-        step_hmax(*pieces[-1])
-        step_out(*pieces[-1])
+        def larger(a):
+            lo, hi = HALVES[a]
+            nc.vector.tensor_tensor(top[LAST][:, lo:hi], last_n7[a][:, lo:hi], last_n8[a][:, lo:hi], ALU.max)
+
+        def finish_direct(a):
+            lo, hi = HALVES[a]
+            nc.vector.scalar_tensor_tensor(result[LAST][:, lo:hi], h_last_bank[:, lo:hi], -0.75, top[LAST][:, lo:hi], ALU.mult, ALU.add)
+            nc.sync.dma_start(out_rows[:, LAST, lo:hi], result[LAST][:, lo:hi])
+
+        fetch(last_n7[0], h_win[LAST], "n7", *HALVES[0])
+        fetch(last_n8[0], h_win[LAST], "n8", *HALVES[0])
+        fetch(last_n7[1], h_win[LAST], "n7", *HALVES[1])
+        larger(0)
+        fetch(last_n8[1], h_win[LAST], "n8", *HALVES[1])
+        finish_direct(0)
+        larger(1)
+        finish_direct(1)

from contextlib import ExitStack

import concourse.mybir as mybir
from concourse.masks import make_identity

K, T, S, N, H = 512, 2048, 512, 512, 512
FLOPS = 2 * S * (3 * K * H + H * N)

F32 = mybir.dt.float32
BF16 = mybir.dt.bfloat16
I32 = mybir.dt.int32
U32 = mybir.dt.uint32
U16 = mybir.dt.uint16
U8 = mybir.dt.uint8
FP8X4 = mybir.dt.float8_e4m3fn_x4
ALU = mybir.AluOpType
ACT = mybir.ActivationFunctionType

P = 128
PACK = 4
BLOCKS = S // P
HALF = S // 2
LAST = PACK - 1
RING = 5
HALVES = ((0, HALF), (HALF, S))
Z_PIECES = ((0, HALF), (HALF, HALF + P), (HALF + P, S))


def tile_picked_triopathbnormbover_none_p_kernel(
    tc, x_words, x_scales, w1, w2, w3, gn, w4, offs, two, three, n1, n2, n3, n4, n5, n6, n7, n8, out
):
    nc = tc.nc
    with ExitStack() as ctx:
        keep = ctx.enter_context(tc.tile_pool(name="keep", bufs=1))
        psum = ctx.enter_context(tc.psum_pool(name="psum", bufs=1))

        def sbuf(name, shape, dtype, on=None):
            return keep.tile(shape, dtype, name=name, tag=on or name, align_bytes=64)

        def tiles(name, width):
            return [sbuf("%s%d" % (name, t), [P, width], F32) for t in range(PACK)]

        banks = [psum.tile([P, S], F32, name="bank%d" % i) for i in range(8)]

        lists, raw = {}, {}

        def load_list(name, ap):
            lists[name] = sbuf("list_" + name, [P, S // 16], U16)
            nc.sync.dma_start(lists[name][:], ap)

        def load_weight(name, ap, parts):
            width = H // parts
            raw[name] = [sbuf("raw_%s_%d" % (name, i), [P, PACK, width], F32) for i in range(parts)]
            for i in range(parts):
                nc.sync.dma_start(raw[name][i][:], ap.rearrange("(p j) c -> p j c", j=PACK)[:, :, width * i : width * (i + 1)])

        scale_table = sbuf("scale_table", [P, T], U8)
        nc.gpsimd.memset(scale_table[:].bitcast(I32), 0)
        for q in range(4):
            nc.sync.dma_start(scale_table[32 * q : 32 * q + 4, :].bitcast(I32), x_scales[0, 4 * q : 4 * q + 4, :].bitcast(I32))
        load_list("offs", offs)
        load_list("two", two)
        load_list("three", three)
        word_table = sbuf("word_table", [P, T], I32)
        nc.sync.dma_start(word_table[:], x_words[0].rearrange("p n t -> p (n t)").bitcast(I32))
        load_weight("w1", w1, 2)
        load_weight("w2", w2, 1)
        load_list("n1", n1)
        load_list("n2", n2)
        load_list("n3", n3)
        load_list("n4", n4)
        load_weight("w3", w3, 1)
        gain = sbuf("gain", [P, PACK], F32)
        nc.sync.dma_start(gain[:], gn.rearrange("(p t) o -> p (t o)", t=PACK))
        load_list("n6", n6)
        load_list("n5", n5)
        load_weight("w4", w4, 1)
        load_list("n7", n7)
        load_list("n8", n8)

        four = sbuf("four", [P, 1], F32)
        one_half = sbuf("one_half", [P, 1], F32)
        nc.gpsimd.memset(four[:], 4.0)
        nc.scalar.activation(one_half[:], four[:], ACT.Abs_reciprocal_sqrt)

        ident = sbuf("ident", [P, P], F32)
        make_identity(nc, ident[:])

        y_win, d_win, b_win = tiles("y_win", 2 * S), tiles("d_win", 2 * S), tiles("b_win", 2 * S)
        m_win = y_win[:LAST] + [sbuf("m_win_last", [P, S], F32)]
        h_win = d_win

        x_code, x_scale, dealt, w_code, w_scale = {}, {}, {}, {}, {}

        def pick_words(name, on=None):
            x_code[name] = sbuf("x_code_" + name, [P, S], U32, on)
            nc.vector.tensor_copy(x_code[name][:], word_table[:].bitcast(U32).indirect(lists[name][:]))

        def pick_scales(name):
            x_scale[name] = sbuf("x_scale_" + name, [P, S], U8)
            nc.vector.tensor_copy(x_scale[name][:], scale_table[:].indirect(lists[name][:]))

        def deal(name, step):
            dealt[name] = sbuf("dealt_" + name, [P, PACK * H], BF16)
            dst = dealt[name][:].rearrange("p (t m j) -> p m j t", t=PACK, j=PACK)
            per_part = P // len(raw[name])
            for m in range(0, P, step):
                src = raw[name][m // per_part][:].rearrange("p j (m t) -> p m j t", t=PACK)
                nc.scalar.copy(dst[:, m : m + step], src[:, m % per_part : m % per_part + step])

        def quantise_weight(name, on=None):
            w_code[name] = sbuf("w_code_" + name, [P, H], U32, on)
            w_scale[name] = sbuf("w_scale_" + name, [P, H], U8)
            nc.vector.quantize_mx(out=w_code[name][:].bitcast(FP8X4), scales=w_scale[name][:], in_=dealt[name][:])

        def block(ap, b):
            return ap[:, P * b : P * (b + 1)]

        def product(dst, w_name, t, codes, scales):
            nc.tensor.matmul_mx(
                out=dst,
                lhsT=block(w_code[w_name], t).bitcast(FP8X4),
                lhsT_scale=block(w_scale[w_name], t),
                rhs=codes.bitcast(FP8X4),
                rhs_scale=scales,
                start=True,
                stop=True,
            )

        def make_y(t, bank):
            product(bank[:], "w1", t, x_code["offs"][:], x_scale["offs"][:])
            nc.scalar.copy(y_win[t][:, :S], bank[:])

        def make_d(t, bank):
            product(bank[:], "w2", t, x_code["two"][:], x_scale["two"][:])
            nc.scalar.copy(d_win[t][:, :S], bank[:])

        def make_abs_b(t, bank):
            product(bank[:], "w3", t, x_code["three"][:], x_scale["three"][:])
            nc.scalar.activation(b_win[t][:, :S], bank[:], ACT.Abs)

        def fetch(dst, win, list_name, lo=0, hi=S):
            nc.vector.tensor_copy(dst[:, lo:hi], win[:].indirect(lists[list_name][:, lo // 16 : hi // 16]))

        def fetch_times(dst, win, list_name, factor, lo=0, hi=S):
            offsets = lists[list_name][:, lo // 16 : hi // 16]
            nc.vector.tensor_scalar(dst[:, lo:hi], win[:].indirect(offsets), factor, 0.0, ALU.mult, ALU.add)

        def turn(dst, src, start, stop):
            nc.tensor.matmul(dst, lhsT=src, rhs=ident[:], start=start, stop=stop, is_transpose=True)

        def add_turned(bank, src, opens, closes):
            for b in range(BLOCKS):
                turn(block(bank, b), block(src, b), opens and b == 0, closes and b == BLOCKS - 1)

        ring = [sbuf("ring%d" % i, [P, S], F32) for i in range(RING)]
        handed_out = []

        def next_in_ring():
            handed_out.append(ring[len(handed_out) % RING])
            return handed_out[-1]

        m_bank, neg_bank, diff_bank = banks[0], banks[2], banks[3]
        base = tiles("base", S)
        rise = [sbuf("rise%d" % t, [P, S], F32) for t in range(LAST)]
        rise_blocks = [[block(rise[t], b) for b in range(BLOCKS)] for t in range(LAST)]
        rise_last = [y_win[1 + a][:, S : S + HALF] for a in range(2)]
        rise_blocks.append([block(rise_last[b // 2], b % 2) for b in range(BLOCKS)])

        def look_up_n1(t):
            g = next_in_ring()
            fetch_times(g, y_win[t], "n1", -1.0)
            add_turned(neg_bank, g, True, False)
            add_turned(diff_bank, g, True, False)

        def look_up_n3(t):
            g = next_in_ring()
            fetch_times(g, d_win[t], "n3", -1.0)
            add_turned(neg_bank, g, False, True)
            add_turned(diff_bank, g, False, False)
            nc.scalar.activation(base[t][:], neg_bank[:], ACT.Copy, scale=-1.0)

        def look_up_n2(t):
            g = next_in_ring()
            fetch(g, y_win[t], "n2")
            add_turned(diff_bank, g, False, False)

        def look_up_n4(t):
            g = next_in_ring()
            fetch(g, d_win[t], "n4")
            add_turned(diff_bank, g, False, True)
            if t < LAST:
                nc.scalar.activation(rise[t][:], diff_bank[:], ACT.Relu)
            else:
                for a, (lo, hi) in enumerate(HALVES):
                    nc.scalar.activation(rise_last[a], diff_bank[:, lo:hi], ACT.Relu)

        def make_gained_m1(t):
            add_turned(m_bank, base[t], True, False)
            for b in range(BLOCKS):
                turn(block(m_bank, b), rise_blocks[t][b], False, b == BLOCKS - 1)
            nc.scalar.activation(m_win[t][:, :S], m_bank[:], ACT.Copy, scale=gain[:, t : t + 1])

        pieces = (HALVES, Z_PIECES)
        num_bank = (banks[4:6], banks[1:4])
        den_bank = banks[6:8]
        unit_bank = banks[4:7]
        root = [[sbuf("root_%d_%d" % (u, a), [P, S], F32) for a in range(2)] for u in range(2)]
        inverse = [[sbuf("inverse_%d_%d" % (u, a), [P, S], F32) for a in range(2)] for u in range(2)]
        z_turned = [[sbuf("z_turned_%d_%d" % (u, i), [P, 2 * (hi - lo)], BF16) for i, (lo, hi) in enumerate(pieces[u])] for u in range(2)]

        def add_to_pair(bank, src, t, lo, hi, opens, closes):
            first, end = lo // P, hi // P
            for b in range(first, end):
                turn(block(bank, 2 * (b - first) + t % 2), block(src, b), opens and b == first, closes and b == end - 1)

        def look_up_n5(t):
            u = t // 2
            for i, (lo, hi) in enumerate(pieces[u]):
                add_to_pair(num_bank[u][i], m_win[t], t, lo, hi, t % 2 == 0, False)
            g = next_in_ring()
            if t < LAST:
                fetch_times(g, m_win[t], "n5", -1.0)
            for i, (lo, hi) in enumerate(pieces[u]):
                if t == LAST:
                    fetch_times(g, m_win[t], "n5", -1.0, lo, hi)
                add_to_pair(num_bank[u][i], g, t, lo, hi, False, t % 2 == 1)

        def look_up_n6(t):
            for a, (lo, hi) in enumerate(HALVES):
                add_to_pair(den_bank[a], b_win[t], t, lo, hi, t % 2 == 0, False)
            g = next_in_ring()
            fetch(g, b_win[t], "n6")
            for a, (lo, hi) in enumerate(HALVES):
                add_to_pair(den_bank[a], g, t, lo, hi, False, t % 2 == 1)
            if t % 2 == 1:
                u = t // 2
                for a in range(2):
                    nc.scalar.activation(
                        root[u][a][:].rearrange("j (b p e) -> j b p e", b=2, e=2),
                        den_bank[a][:].rearrange("j (b e p) -> j b p e", b=2, e=2),
                        ACT.Abs_reciprocal_sqrt,
                        bias=one_half[:],
                    )
                    nc.scalar.activation(inverse[u][a][:], root[u][a][:], ACT.Square)

        def form_z(u, i):
            lo, hi = pieces[u][i]
            count, first = 2 * (hi - lo), 2 * (lo % HALF)
            nc.vector.tensor_tensor(
                z_turned[u][i][:].rearrange("j (b p e) -> j b p e", p=P, e=2),
                num_bank[u][i][:, :count].rearrange("j (b e p) -> j b p e", p=P, e=2),
                inverse[u][lo // HALF][:, first : first + count].rearrange("j (b p e) -> j b p e", p=P, e=2),
                ALU.mult,
            )

        def turn_z_back(u, i):
            lo, hi = pieces[u][i]
            units = z_turned[u][i][:].bitcast(F32)
            for b in range(lo // P, hi // P):
                k = [z_lo <= P * b < z_hi for z_lo, z_hi in Z_PIECES].index(True)
                z_lo, z_hi = Z_PIECES[k]
                turn(block(unit_bank[k], u * ((z_hi - z_lo) // P) + b - z_lo // P), block(units, b - lo // P), True, True)

        for name in ("offs", "two", "three"):
            pick_scales(name)
        pick_words("offs")
        pick_words("two")
        deal("w1", P // 2)
        quantise_weight("w1")
        pick_words("three", on="raw_w1_1")

        make_y(0, banks[0])
        deal("w2", P // 4)
        look_up_n1(0)
        quantise_weight("w2")
        make_d(0, banks[1])
        make_y(1, banks[4])
        look_up_n2(0)
        look_up_n3(0)
        make_d(1, banks[7])
        look_up_n4(0)
        deal("w3", P // 2)
        make_y(2, banks[5])
        make_d(2, banks[0])
        look_up_n1(1)
        make_gained_m1(0)
        look_up_n3(1)
        quantise_weight("w3")
        make_abs_b(0, banks[1])
        make_y(3, banks[6])
        make_d(3, banks[4])
        make_abs_b(1, banks[7])
        look_up_n2(1)
        look_up_n4(1)
        make_abs_b(2, banks[5])
        make_abs_b(3, banks[1])
        look_up_n6(0)
        make_gained_m1(1)

        look_up_n1(2)
        look_up_n3(2)
        look_up_n5(0)
        look_up_n2(2)
        look_up_n4(2)
        look_up_n6(1)
        make_gained_m1(2)
        look_up_n1(3)
        deal("w4", P // 2)
        look_up_n3(3)
        look_up_n2(3)
        look_up_n4(3)
        look_up_n6(2)
        make_gained_m1(3)

        look_up_n6(3)
        for t in range(1, PACK):
            look_up_n5(t)
        for a in range(2):
            form_z(0, a)
        for a in range(2):
            turn_z_back(0, a)

        z_rows = [sbuf("z_rows%d" % i, [P, PACK * (hi - lo)], BF16) for i, (lo, hi) in enumerate(Z_PIECES)]
        z_code = sbuf("z_code", [P, S], U32)
        z_scale = sbuf("z_scale", [P, S], U8)
        for i, (lo, hi) in enumerate(Z_PIECES):
            form_z(1, i)
            turn_z_back(1, i)
            nc.scalar.copy(
                z_rows[i][:].bitcast(F32).rearrange("p (j u) -> p j u", u=2),
                unit_bank[i][:, : 2 * (hi - lo)].rearrange("p (u j) -> p j u", u=2),
            )
        quantise_weight("w4", on="inverse_1_1")

        h_first_bank = [banks[0], banks[7], banks[1]]
        for i, (lo, hi) in enumerate(Z_PIECES):
            nc.vector.quantize_mx(out=z_code[:, lo:hi].bitcast(FP8X4), scales=z_scale[:, lo:hi], in_=z_rows[i][:])
            product(h_first_bank[i][:, : hi - lo], "w4", 0, z_code[:, lo:hi], z_scale[:, lo:hi])
            nc.scalar.copy(h_win[0][:, lo:hi], h_first_bank[i][:, : hi - lo])
        for t in range(1, PACK):
            product(banks[1 + t][:], "w4", t, z_code[:], z_scale[:])
            nc.scalar.copy(h_win[t][:, :S], banks[1 + t][:])
        h_last_bank = banks[1 + LAST]

        out_rows = out.rearrange("(p t) j -> p t j", t=PACK)
        low_bank = [banks[0], banks[1], banks[3]]
        gap_bank = [banks[7], banks[2], banks[7]]
        out_bank = [banks[5], banks[6], banks[5]]
        top, result = tiles("top", S), tiles("result", S)

        def finish_turned(t):
            add_turned(out_bank[t], top[t], False, True)
            nc.scalar.copy(result[t][:], out_bank[t][:])
            nc.scalar.dma_start(out_rows[:, t, :], result[t][:])

        for t in range(LAST):
            at_n7 = sbuf("at_n7_%d" % t, [P, S], F32)
            fetch_times(at_n7, h_win[t], "n7", -4.0 / 3.0)
            add_turned(low_bank[t], h_win[t], True, False)
            add_turned(low_bank[t], at_n7, False, True)
            add_turned(gap_bank[t], at_n7, True, False)
            nc.scalar.activation(base[t][:], low_bank[t][:], ACT.Copy, scale=-0.75)
            add_turned(out_bank[t], base[t], True, False)
            at_n8 = sbuf("at_n8_%d" % t, [P, S], F32)
            fetch_times(at_n8, h_win[t], "n8", 4.0 / 3.0)
            add_turned(gap_bank[t], at_n8, False, True)
            nc.scalar.activation(top[t][:], gap_bank[t][:], ACT.Relu, scale=0.75)
            if t > 0:
                finish_turned(t - 1)
        finish_turned(LAST - 1)

        last_n7 = [sbuf("last_n7_%d" % a, [P, S], F32) for a in range(2)]
        last_n8 = [sbuf("last_n8_%d" % a, [P, S], F32) for a in range(2)]

        def larger(a):
            lo, hi = HALVES[a]
            nc.vector.tensor_tensor(top[LAST][:, lo:hi], last_n7[a][:, lo:hi], last_n8[a][:, lo:hi], ALU.max)

        def finish_direct(a):
            lo, hi = HALVES[a]
            nc.vector.scalar_tensor_tensor(result[LAST][:, lo:hi], h_last_bank[:, lo:hi], -0.75, top[LAST][:, lo:hi], ALU.mult, ALU.add)
            nc.sync.dma_start(out_rows[:, LAST, lo:hi], result[LAST][:, lo:hi])

        fetch(last_n7[0], h_win[LAST], "n7", *HALVES[0])
        fetch(last_n8[0], h_win[LAST], "n8", *HALVES[0])
        fetch(last_n7[1], h_win[LAST], "n7", *HALVES[1])
        larger(0)
        fetch(last_n8[1], h_win[LAST], "n8", *HALVES[1])
        finish_direct(0)
        larger(1)
        finish_direct(1)
